import numpy as np, ml_dtypes
CORES = [10,14,66,70,74,78,82,86,90,94,106,110]
N = 12
TK = 256
def setup_inputs(rng):
    return {"x": rng.standard_normal((N, 128, TK), dtype=np.float32).astype(ml_dtypes.bfloat16), "w1": (rng.standard_normal((N, 128, 128), dtype=np.float32) / 8).astype(ml_dtypes.bfloat16), "w2": (rng.standard_normal((N, 128, 128), dtype=np.float32) / 8).astype(ml_dtypes.bfloat16)}
def setup_inputs_big(rng):
    d = setup_inputs(rng)
    for k in ("x", "w1", "w2"): d[k] = (d[k].astype(np.float32) * 1024.0).astype(d[k].dtype)
    return d
def setup_inputs_small(rng):
    d = setup_inputs(rng)
    for k in ("x", "w1", "w2"): d[k] = (d[k].astype(np.float32) * (1 / 1024.0)).astype(d[k].dtype)
    return d
def setup_inputs_apart(rng):
    d = setup_inputs(rng)
    f = (10.0 ** rng.permutation(np.linspace(-1.5, 1.5, N))).astype(np.float32).reshape(N, 1, 1)
    for k in ("x", "w1", "w2"): d[k] = (d[k].astype(np.float32) * f).astype(d[k].dtype)
    return d
def reference(x, w1, w2):
    X, W1, W2 = x.astype(np.float64), w1.astype(np.float64), w2.astype(np.float64)
    y = np.zeros((N, 128, TK))
    for r in range(N):
        for j in range(N):
            y[r] += W2[j].T @ np.maximum(W1[j].T @ X[r], 0.0)
    return {"y": y.astype(ml_dtypes.bfloat16 if x.dtype != np.float64 else np.float64)}

@@ -1,0 +1,128 @@
+from concourse.bass import DstId, RemoteDMATransfer
+from concourse.mybir import AluOpType
+
+N = 12
+TK = 256
+DM = 128
+WW = 2 * DM
+
+SCRATCH = {
+    "wall": ("sbuf", [128, N * WW], "bfloat16"),
+    "xx": ("sbuf", [128, 2 * TK], "bfloat16"),
+    "zero": ("sbuf", [128, TK], "bfloat16"),
+    "h0": ("sbuf", [128, TK], "bfloat16"),
+    "h1": ("sbuf", [128, TK], "bfloat16"),
+    "ysend": ("sbuf", [128, TK], "bfloat16"),
+    "yland": ("sbuf", [128, TK], "bfloat16"),
+    "yout": ("sbuf", [128, TK], "bfloat16"),
+    "ph0": ("psum", [128, 512], "float32"),
+    "ph1": ("psum", [128, 512], "float32"),
+    "acc0": ("psum", [128, 512], "float32"),
+    "acc1": ("psum", [128, 512], "float32"),
+}
+SEMAPHORES = ["ldw", "ldx", "zed", "xarr", "yarr", "loc", "cp", "add", "st",
+              "mm1_0", "mm1_1", "relu_0", "relu_1", "mm2_0", "mm2_1"] + ["arr%d" % r for r in range(N)]
+
+
+def _bits(mask):
+    return bin(mask).count("1")
+
+
+def rank_program(g, core, T, topo):
+    rank = T.rank_of(core)
+    if rank is None:
+        return
+    S = T.sem
+    cores = list(T.cores)
+    chips = sorted({topo.chip(c) for c in cores})
+    nch = len(chips)
+    me = chips.index(topo.chip(core))
+    my_die = topo.die(core)
+
+    def at(ci, same_die):
+        return [c for c in cores if topo.chip(c) == chips[ci % nch] and (topo.die(c) == my_die) == same_die][0]
+
+    partner = at(me, False)
+    sends = [at(me + s, True) for s in range(1, nch)]
+    froms = [at(me - s, True) for s in range(1, nch)]
+    off_mask = topo.mask(core, sends[0])
+    all_mask = topo.mask(core, partner)
+    on_mask = all_mask & ~off_mask
+    n_off, n_on, n_all = _bits(off_mask), _bits(on_mask), _bits(all_mask)
+
+    def slot(r):
+        return r * WW
+
+    own = slot(rank)
+    OWN, PAR = 0, 1
+    PH, ACC, H = [T.ph0, T.ph1], [T.acc0, T.acc1], [T.h0, T.h1]
+    MM1, RELU, MM2 = [S.mm1_0, S.mm1_1], [S.relu_0, S.relu_1], [S.mm2_0, S.mm2_1]
+
+    g.sync.dma_start(T.wall[:, own:own + DM], T.w1[:]).then_inc(S.ldw, 16)
+    g.scalar.dma_start(T.wall[:, own + DM:own + WW], T.w2[:]).then_inc(S.ldw, 16)
+    g.sync.dma_start(T.xx[0:64, 0:TK], T.x[0:64, :]).then_inc(S.ldx, 16)
+    g.scalar.dma_start(T.xx[64:128, 0:TK], T.x[64:128, :]).then_inc(S.ldx, 16)
+
+    g.wait_ge(S.ldw, 32)
+    ids = []
+    for d in sends:
+        rid, pid, _ = topo.addr(d)
+        ids.append(DstId(rid=rid, pnc=pid))
+    g.remote_dma_fused([RemoteDMATransfer(dst_ids=ids, dma_engine_mask=off_mask, remote_sem=S["arr%d" % rank],
+                                          srcs=[T.wall[:, own:own + WW]],
+                                          dsts=[T.wall[:, own:own + WW] for _ in sends])], local_sem=S.loc)
+    prid, ppid, _ = topo.addr(partner)
+    g.wait_ge(S.ldx, 32)
+    g.remote_dma(out_ap=T.xx[:, TK:2 * TK], in_ap=T.xx[:, 0:TK], remote_sem=S.xarr, local_sem=S.loc,
+                 pid=ppid, routing_id=prid, dma_engine_mask=on_mask)
+    g.wait_ge(S.cp, 1)
+    g.remote_dma(out_ap=T.yland[:], in_ap=T.ysend[:], remote_sem=S.yarr, local_sem=S.loc,
+                 pid=ppid, routing_id=prid, dma_engine_mask=all_mask)
+    g.wait_ge(S.loc, n_off + n_on + n_all)
+
+    work = [(rank, [OWN, PAR])] + [(T.rank_of(c), [PAR, OWN]) for c in froms]
+    total = [sum(1 for _, hs in work if h in hs) for h in (OWN, PAR)]
+
+    t = g.tensor
+    seen = [0, 0]
+    for r, hs in work:
+        if r == rank:
+            t.wait_ge(S.ldw, 32)
+        else:
+            t.wait_ge(S["arr%d" % r], n_off)
+        c0 = slot(r)
+        for h in hs:
+            if seen[h] == 0:
+                if h == OWN:
+                    t.wait_ge(S.ldx, 32)
+                else:
+                    t.wait_ge(S.xarr, n_on)
+            t.matmul(PH[h][:, 0:TK], T.wall[:, c0:c0 + DM], T.xx[:, h * TK:(h + 1) * TK],
+                     start=True, stop=True).then_inc(MM1[h], 1)
+        for h in hs:
+            seen[h] += 1
+            t.wait_ge(RELU[h], seen[h])
+            t.matmul(ACC[h][:, 0:TK], T.wall[:, c0 + DM:c0 + WW], H[h][:],
+                     start=(seen[h] == 1), stop=(seen[h] == total[h])).then_inc(MM2[h], 1)
+
+    v = g.vector
+    v.memset(T.zero[:], 0.0).then_inc(S.zed, 1)
+    v.wait_ge(S.zed, 1)
+    done = [0, 0]
+    for r, hs in work:
+        for h in hs:
+            done[h] += 1
+            v.wait_ge(MM1[h], done[h])
+            if done[h] > 1:
+                v.wait_ge(MM2[h], done[h] - 1)
+            v.tensor_tensor(out=H[h][:], in0=PH[h][:, 0:TK], in1=T.zero[:], op=AluOpType.max).then_inc(RELU[h], 1)
+            if h == PAR and done[h] == total[h]:
+                v.wait_ge(MM2[h], total[h])
+                v.tensor_copy(out=T.ysend[:], in_=ACC[h][:, 0:TK]).then_inc(S.cp, 1)
+    v.wait_ge(MM2[OWN], total[OWN])
+    v.wait_ge(S.yarr, n_all)
+    v.tensor_tensor(out=T.yout[:], in0=ACC[OWN][:, 0:TK], in1=T.yland[:], op=AluOpType.add).then_inc(S.add, 1)
+
+    g.sync.wait_ge(S.add, 1)
+    g.sync.dma_start(T.y[:], T.yout[:]).then_inc(S.st, 16)
+    g.sync.wait_ge(S.st, 16)

@@ -35,23 +35,45 @@ def rank_program(g, core, T, topo):
     S = T.sem
     cores = list(T.cores)
     chips = sorted({topo.chip(c) for c in cores})
-    nch = len(chips)
-    me = chips.index(topo.chip(core))
-    my_die = topo.die(core)
+    n = len(chips)
+    m = n - 1
 
-    def at(ci, same_die):
-        return [c for c in cores if topo.chip(c) == chips[ci % nch] and (topo.die(c) == my_die) == same_die][0]
+    tw = {}
+    for a in chips:
+        for b in chips:
+            if topo.mates(a, b):
+                tw[a] = b
+    rest = [a for a in chips if a not in tw]
+    for i in range(0, len(rest), 2):
+        tw[rest[i]], tw[rest[i + 1]] = rest[i + 1], rest[i]
+    pairs = sorted({(min(a, tw[a]), max(a, tw[a])) for a in chips})
+    lab = [None] * n
+    lab[m], lab[0] = pairs[0]
+    for k in range(1, n // 2):
+        lab[k], lab[m - k] = pairs[k]
 
-    partner = at(me, False)
-    sends = [at(me + s, True) for s in range(1, nch)]
-    froms = [at(me - s, True) for s in range(1, nch)]
+    def peer(ch, r):
+        p = lab.index(ch)
+        return lab[r if p == m else (m if p == r else (2 * r - p) % m)]
+
+    def rank_at(ch, die):
+        return [c for c in cores if topo.chip(c) == ch and topo.die(c) == die][0]
+
+    def other(c):
+        return [d for d in cores if topo.chip(d) == topo.chip(c) and d != c][0]
+
+    def slot(r):
+        return r * WW
+
+    my_chip, my_die = topo.chip(core), topo.die(core)
+    partner = other(core)
+    steps = [rank_at(peer(my_chip, r), my_die) for r in list(range(1, m)) + [0]]
+    cross = other(steps[-1])
+    sends = steps[:-1] + [cross, steps[-1]]
     off_mask = topo.mask(core, sends[0])
     all_mask = topo.mask(core, partner)
     on_mask = all_mask & ~off_mask
     n_off, n_on, n_all = _bits(off_mask), _bits(on_mask), _bits(all_mask)
-
-    def slot(r):
-        return r * WW
 
     own = slot(rank)
     OWN, PAR = 0, 1
@@ -77,50 +99,75 @@ def rank_program(g, core, T, topo):
                  pid=ppid, routing_id=prid, dma_engine_mask=on_mask)
     g.wait_ge(S.cp, 1)
     g.remote_dma(out_ap=T.yland[:], in_ap=T.ysend[:], remote_sem=S.yarr, local_sem=S.loc,
-                 pid=ppid, routing_id=prid, dma_engine_mask=all_mask)
-    g.wait_ge(S.loc, n_off + n_on + n_all)
+                 pid=ppid, routing_id=prid, dma_engine_mask=on_mask)
+    g.wait_ge(S.loc, n_off + 2 * n_on)
 
-    work = [(rank, [OWN, PAR])] + [(T.rank_of(c), [PAR, OWN]) for c in froms]
-    total = [sum(1 for _, hs in work if h in hs) for h in (OWN, PAR)]
+    tasks, ops = [], []
+
+    def task(r, half, c0, w, b):
+        tasks.append((r, half, c0, w, b))
+        return len(tasks) - 1
+
+    HF = TK // 2
+    a, b = task(rank, OWN, 0, TK, 0), task(rank, PAR, 0, TK, 1)
+    ops += [("w", S.ldw, 32), ("w", S.ldx, 32), ("1", a), ("w", S.xarr, n_on), ("1", b), ("2", a), ("2", b)]
+    for c in steps[:-2]:
+        r = T.rank_of(c)
+        p, o = task(r, PAR, 0, TK, 1), task(r, OWN, 0, TK, 0)
+        ops += [("w", S["arr%d" % r], n_off), ("1", p), ("1", o), ("2", p), ("2", o)]
+    r = T.rank_of(steps[-2])
+    pa, pb = task(r, PAR, 0, HF, 0), task(r, PAR, HF, HF, 1)
+    last_par = pb
+    ops += [("w", S["arr%d" % r], n_off), ("1", pa), ("1", pb), ("2", pa), ("2", pb)]
+    o4 = task(r, OWN, 0, TK, 0)
+    ra = T.rank_of(cross)
+    ta = task(ra, OWN, 0, TK, 1)
+    ops += [("1", o4), ("w", S["arr%d" % ra], n_off), ("1", ta), ("2", o4), ("2", ta)]
+    rb = T.rank_of(steps[-1])
+    ba, bb = task(rb, OWN, 0, HF, 0), task(rb, OWN, HF, HF, 1)
+    ops += [("w", S["arr%d" % rb], n_off), ("1", ba), ("1", bb), ("2", ba), ("2", bb)]
+
+    cnt = [0, 0]
+    ordn = []
+    for (_, _, _, _, bf) in tasks:
+        cnt[bf] += 1
+        ordn.append(cnt[bf])
+    seconds = [op[1] for op in ops if op[0] == "2"]
+    first2 = {h: [k for k in seconds if tasks[k][1] == h][0] for h in (OWN, PAR)}
+    last2 = {h: [k for k in seconds if tasks[k][1] == h][-1] for h in (OWN, PAR)}
 
     t = g.tensor
-    seen = [0, 0]
-    for r, hs in work:
-        if r == rank:
-            t.wait_ge(S.ldw, 32)
+    for op in ops:
+        if op[0] == "w":
+            t.wait_ge(op[1], op[2])
+            continue
+        k = op[1]
+        r, half, c0, w, bf = tasks[k]
+        w0 = slot(r)
+        if op[0] == "1":
+            t.matmul(PH[bf][:, 0:w], T.wall[:, w0:w0 + DM], T.xx[:, half * TK + c0:half * TK + c0 + w],
+                     start=True, stop=True).then_inc(MM1[bf], 1)
         else:
-            t.wait_ge(S["arr%d" % r], n_off)
-        c0 = slot(r)
-        for h in hs:
-            if seen[h] == 0:
-                if h == OWN:
-                    t.wait_ge(S.ldx, 32)
-                else:
-                    t.wait_ge(S.xarr, n_on)
-            t.matmul(PH[h][:, 0:TK], T.wall[:, c0:c0 + DM], T.xx[:, h * TK:(h + 1) * TK],
-                     start=True, stop=True).then_inc(MM1[h], 1)
-        for h in hs:
-            seen[h] += 1
-            t.wait_ge(RELU[h], seen[h])
-            t.matmul(ACC[h][:, 0:TK], T.wall[:, c0 + DM:c0 + WW], H[h][:],
-                     start=(seen[h] == 1), stop=(seen[h] == total[h])).then_inc(MM2[h], 1)
+            t.wait_ge(RELU[bf], ordn[k])
+            t.matmul(ACC[half][:, c0:c0 + w], T.wall[:, w0 + DM:w0 + WW], H[bf][:, 0:w],
+                     start=(k == first2[half]), stop=(k == last2[half])).then_inc(MM2[bf], 1)
 
     v = g.vector
     v.memset(T.zero[:], 0.0).then_inc(S.zed, 1)
     v.wait_ge(S.zed, 1)
-    done = [0, 0]
-    for r, hs in work:
-        for h in hs:
-            done[h] += 1
-            v.wait_ge(MM1[h], done[h])
-            if done[h] > 1:
-                v.wait_ge(MM2[h], done[h] - 1)
-            v.tensor_tensor(out=H[h][:], in0=PH[h][:, 0:TK], in1=T.zero[:], op=AluOpType.max).then_inc(RELU[h], 1)
-            if h == PAR and done[h] == total[h]:
-                v.wait_ge(MM2[h], total[h])
-                v.tensor_copy(out=T.ysend[:], in_=ACC[h][:, 0:TK]).then_inc(S.cp, 1)
-    v.wait_ge(MM2[OWN], total[OWN])
-    v.wait_ge(S.yarr, n_all)
+    for k, (r, half, c0, w, bf) in enumerate(tasks):
+        v.wait_ge(MM1[bf], ordn[k])
+        if ordn[k] > 1:
+            v.wait_ge(MM2[bf], ordn[k] - 1)
+        v.tensor_tensor(out=H[bf][:, 0:w], in0=PH[bf][:, 0:w], in1=T.zero[:, 0:w],
+                        op=AluOpType.max).then_inc(RELU[bf], 1)
+        if k == last_par:
+            v.wait_ge(MM2[tasks[pa][4]], ordn[pa])
+            v.wait_ge(MM2[tasks[pb][4]], ordn[pb])
+            v.tensor_copy(out=T.ysend[:], in_=ACC[PAR][:, 0:TK]).then_inc(S.cp, 1)
+    v.wait_ge(MM2[0], cnt[0])
+    v.wait_ge(MM2[1], cnt[1])
+    v.wait_ge(S.yarr, n_on)
     v.tensor_tensor(out=T.yout[:], in0=ACC[OWN][:, 0:TK], in1=T.yland[:], op=AluOpType.add).then_inc(S.add, 1)
 
     g.sync.wait_ge(S.add, 1)

from concourse.bass import DstId, RemoteDMATransfer
from concourse.mybir import AluOpType

N = 12
TK = 256
DM = 128
WW = 2 * DM

SCRATCH = {
    "wall": ("sbuf", [128, N * WW], "bfloat16"),
    "xx": ("sbuf", [128, 2 * TK], "bfloat16"),
    "zero": ("sbuf", [128, TK], "bfloat16"),
    "h0": ("sbuf", [128, TK], "bfloat16"),
    "h1": ("sbuf", [128, TK], "bfloat16"),
    "ysend": ("sbuf", [128, TK], "bfloat16"),
    "yland": ("sbuf", [128, TK], "bfloat16"),
    "yout": ("sbuf", [128, TK], "bfloat16"),
    "ph0": ("psum", [128, 512], "float32"),
    "ph1": ("psum", [128, 512], "float32"),
    "acc0": ("psum", [128, 512], "float32"),
    "acc1": ("psum", [128, 512], "float32"),
}
SEMAPHORES = ["ldw", "ldx", "zed", "xarr", "yarr", "loc", "cp", "add", "st",
              "mm1_0", "mm1_1", "relu_0", "relu_1", "mm2_0", "mm2_1"] + ["arr%d" % r for r in range(N)]


def _bits(mask):
    return bin(mask).count("1")


def rank_program(g, core, T, topo):
    rank = T.rank_of(core)
    if rank is None:
        return
    S = T.sem
    cores = list(T.cores)
    chips = sorted({topo.chip(c) for c in cores})
    n = len(chips)
    m = n - 1

    tw = {}
    for a in chips:
        for b in chips:
            if topo.mates(a, b):
                tw[a] = b
    rest = [a for a in chips if a not in tw]
    for i in range(0, len(rest), 2):
        tw[rest[i]], tw[rest[i + 1]] = rest[i + 1], rest[i]
    pairs = sorted({(min(a, tw[a]), max(a, tw[a])) for a in chips})
    lab = [None] * n
    lab[m], lab[0] = pairs[0]
    for k in range(1, n // 2):
        lab[k], lab[m - k] = pairs[k]

    def peer(ch, r):
        p = lab.index(ch)
        return lab[r if p == m else (m if p == r else (2 * r - p) % m)]

    def rank_at(ch, die):
        return [c for c in cores if topo.chip(c) == ch and topo.die(c) == die][0]

    def other(c):
        return [d for d in cores if topo.chip(d) == topo.chip(c) and d != c][0]

    def slot(r):
        return r * WW

    my_chip, my_die = topo.chip(core), topo.die(core)
    partner = other(core)
    steps = [rank_at(peer(my_chip, r), my_die) for r in list(range(1, m)) + [0]]
    cross = other(steps[-1])
    sends = steps[:-1] + [cross, steps[-1]]
    off_mask = topo.mask(core, sends[0])
    all_mask = topo.mask(core, partner)
    on_mask = all_mask & ~off_mask
    n_off, n_on, n_all = _bits(off_mask), _bits(on_mask), _bits(all_mask)

    own = slot(rank)
    OWN, PAR = 0, 1
    PH, ACC, H = [T.ph0, T.ph1], [T.acc0, T.acc1], [T.h0, T.h1]
    MM1, RELU, MM2 = [S.mm1_0, S.mm1_1], [S.relu_0, S.relu_1], [S.mm2_0, S.mm2_1]

    g.sync.dma_start(T.wall[:, own:own + DM], T.w1[:]).then_inc(S.ldw, 16)
    g.scalar.dma_start(T.wall[:, own + DM:own + WW], T.w2[:]).then_inc(S.ldw, 16)
    g.sync.dma_start(T.xx[0:64, 0:TK], T.x[0:64, :]).then_inc(S.ldx, 16)
    g.scalar.dma_start(T.xx[64:128, 0:TK], T.x[64:128, :]).then_inc(S.ldx, 16)

    g.wait_ge(S.ldw, 32)
    ids = []
    for d in sends:
        rid, pid, _ = topo.addr(d)
        ids.append(DstId(rid=rid, pnc=pid))
    g.remote_dma_fused([RemoteDMATransfer(dst_ids=ids, dma_engine_mask=off_mask, remote_sem=S["arr%d" % rank],
                                          srcs=[T.wall[:, own:own + WW]],
                                          dsts=[T.wall[:, own:own + WW] for _ in sends])], local_sem=S.loc)
    prid, ppid, _ = topo.addr(partner)
    g.wait_ge(S.ldx, 32)
    g.remote_dma(out_ap=T.xx[:, TK:2 * TK], in_ap=T.xx[:, 0:TK], remote_sem=S.xarr, local_sem=S.loc,
                 pid=ppid, routing_id=prid, dma_engine_mask=on_mask)
    g.wait_ge(S.cp, 1)
    g.remote_dma(out_ap=T.yland[:], in_ap=T.ysend[:], remote_sem=S.yarr, local_sem=S.loc,
                 pid=ppid, routing_id=prid, dma_engine_mask=on_mask)
    g.wait_ge(S.loc, n_off + 2 * n_on)

    tasks, ops = [], []

    def task(r, half, c0, w, b):
        tasks.append((r, half, c0, w, b))
        return len(tasks) - 1

    HF = TK // 2
    a, b = task(rank, OWN, 0, TK, 0), task(rank, PAR, 0, TK, 1)
    ops += [("w", S.ldw, 32), ("w", S.ldx, 32), ("1", a), ("w", S.xarr, n_on), ("1", b), ("2", a), ("2", b)]
    for c in steps[:-2]:
        r = T.rank_of(c)
        p, o = task(r, PAR, 0, TK, 1), task(r, OWN, 0, TK, 0)
        ops += [("w", S["arr%d" % r], n_off), ("1", p), ("1", o), ("2", p), ("2", o)]
    r = T.rank_of(steps[-2])
    pa, pb = task(r, PAR, 0, HF, 0), task(r, PAR, HF, HF, 1)
    last_par = pb
    ops += [("w", S["arr%d" % r], n_off), ("1", pa), ("1", pb), ("2", pa), ("2", pb)]
    o4 = task(r, OWN, 0, TK, 0)
    ra = T.rank_of(cross)
    ta = task(ra, OWN, 0, TK, 1)
    ops += [("1", o4), ("w", S["arr%d" % ra], n_off), ("1", ta), ("2", o4), ("2", ta)]
    rb = T.rank_of(steps[-1])
    ba, bb = task(rb, OWN, 0, HF, 0), task(rb, OWN, HF, HF, 1)
    ops += [("w", S["arr%d" % rb], n_off), ("1", ba), ("1", bb), ("2", ba), ("2", bb)]

    cnt = [0, 0]
    ordn = []
    for (_, _, _, _, bf) in tasks:
        cnt[bf] += 1
        ordn.append(cnt[bf])
    seconds = [op[1] for op in ops if op[0] == "2"]
    first2 = {h: [k for k in seconds if tasks[k][1] == h][0] for h in (OWN, PAR)}
    last2 = {h: [k for k in seconds if tasks[k][1] == h][-1] for h in (OWN, PAR)}

    t = g.tensor
    for op in ops:
        if op[0] == "w":
            t.wait_ge(op[1], op[2])
            continue
        k = op[1]
        r, half, c0, w, bf = tasks[k]
        w0 = slot(r)
        if op[0] == "1":
            t.matmul(PH[bf][:, 0:w], T.wall[:, w0:w0 + DM], T.xx[:, half * TK + c0:half * TK + c0 + w],
                     start=True, stop=True).then_inc(MM1[bf], 1)
        else:
            t.wait_ge(RELU[bf], ordn[k])
            t.matmul(ACC[half][:, c0:c0 + w], T.wall[:, w0 + DM:w0 + WW], H[bf][:, 0:w],
                     start=(k == first2[half]), stop=(k == last2[half])).then_inc(MM2[bf], 1)

    v = g.vector
    v.memset(T.zero[:], 0.0).then_inc(S.zed, 1)
    v.wait_ge(S.zed, 1)
    for k, (r, half, c0, w, bf) in enumerate(tasks):
        v.wait_ge(MM1[bf], ordn[k])
        if ordn[k] > 1:
            v.wait_ge(MM2[bf], ordn[k] - 1)
        v.tensor_tensor(out=H[bf][:, 0:w], in0=PH[bf][:, 0:w], in1=T.zero[:, 0:w],
                        op=AluOpType.max).then_inc(RELU[bf], 1)
        if k == last_par:
            v.wait_ge(MM2[tasks[pa][4]], ordn[pa])
            v.wait_ge(MM2[tasks[pb][4]], ordn[pb])
            v.tensor_copy(out=T.ysend[:], in_=ACC[PAR][:, 0:TK]).then_inc(S.cp, 1)
    v.wait_ge(MM2[0], cnt[0])
    v.wait_ge(MM2[1], cnt[1])
    v.wait_ge(S.yarr, n_on)
    v.tensor_tensor(out=T.yout[:], in0=ACC[OWN][:, 0:TK], in1=T.yland[:], op=AluOpType.add).then_inc(S.add, 1)

    g.sync.wait_ge(S.add, 1)
    g.sync.dma_start(T.y[:], T.yout[:]).then_inc(S.st, 16)
    g.sync.wait_ge(S.st, 16)
